import numpy as np
import ml_dtypes


def mxq(x, axis, fmt="e4m3"):
    dtype, down = {"e4m3": (ml_dtypes.float8_e4m3fn, 7), "e5m2": (ml_dtypes.float8_e5m2, 14)}[fmt]
    v = np.moveaxis(np.asarray(x, np.float32).astype(ml_dtypes.bfloat16).astype(np.float64), axis, -1)
    blocks = v.reshape(v.shape[:-1] + (-1, 32))
    amax = np.abs(blocks).max(-1, keepdims=True)
    byte = np.maximum(np.where(amax > 0, np.frexp(amax)[1] - 1 + 127, 0) - down, 1)
    scale = np.exp2(byte - 127.0)
    codes = (blocks / scale).astype(np.float32).astype(dtype).astype(np.float64)
    return np.moveaxis((codes * scale).reshape(v.shape), -1, axis)


WIDE = False


def mx_kscale(k):
    if not WIDE:
        return np.ones(k)
    levels = np.array([10, -10, 5, -5, 0])
    if k % 512:
        return np.exp2(np.random.permutation(np.resize(levels, k // 32))).repeat(32)
    a = np.empty((k // 512, 16))
    for p in range(k // 512):
        a[p, :8] = np.random.permutation(np.resize(levels, 8))
        for g in range(8):
            far = levels[np.abs(levels - a[p, g]) >= 10]
            a[p, g + 8] = far[np.random.randint(len(far))]
    return np.exp2(a.ravel()).repeat(32)


def f64(x):
    return np.asarray(x).astype(np.float64)


def striped(idx):
    return np.tile(idx.reshape(-1, 16).T, (8, 1)).astype(np.uint16)


def unstriped(offs):
    return offs[:16].T.reshape(-1).astype(np.int64)


def pack_weight(w):
    k, n = w.shape
    w = f64(np.asarray(w, np.float32).astype(ml_dtypes.bfloat16)).reshape(k // 32, 32, n)
    amax = np.abs(w).max(1)
    byte = np.clip(np.where(amax > 0, np.frexp(amax)[1] - 1 + 127 - 7, 1), 1, 254)
    scaled = (w * np.exp2(127.0 - byte)[:, None, :]).reshape(k, n).astype(np.float32)
    words = np.ascontiguousarray(scaled.reshape(k // 512, 128, 4, n).transpose(0, 1, 3, 2)).astype(ml_dtypes.float8_e4m3fn).view(np.uint8)
    return words, np.ascontiguousarray(byte.astype(np.uint8).reshape(k // 512, 16, n))


def unpack_weight(words, scales):
    g, p, n, _ = words.shape
    vals = np.ascontiguousarray(words).view(ml_dtypes.float8_e4m3fn).astype(np.float64) * np.repeat(np.exp2(scales.astype(np.float64) - 127.0), 8, axis=1)[..., None]
    return vals.transpose(0, 1, 3, 2).reshape(g * 512, n)


def relu(v):
    return np.maximum(v, 0.0)


K, T, D, S, V, N = 1024, 512, 8, 2048, 256, 512


def setup_inputs():
    n = np.random.standard_normal
    s = mx_kscale(K)[:, None]
    words, scales = pack_weight(n((K, N)) / np.sqrt(K) / s)
    return {
        "xT": (n((K, T)) * s).astype(np.float32),
        "w_words": words,
        "w_scales": scales,
        "b": (0.3 * n((N, 1))).astype(np.float32),
        "gate": np.tile(np.random.uniform(0.2, 1.0, (D, 1, V)) / np.sqrt(D), (1, N, 1)).astype(np.float32),
        "pos1": striped(np.random.permutation(T)[:V]),
        "pos2": striped(np.random.permutation(T)[:V]),
        "pos3": striped(np.random.permutation(T)[:V]),
        "pos4": striped(np.random.permutation(T)[:V]),
        "pos5": striped(np.random.permutation(T)[:V]),
        "pos6": striped(np.random.permutation(T)[:V]),
        "pos7": striped(np.random.permutation(T)[:V]),
        "pos8": striped(np.random.permutation(T)[:V]),
    }


def reference(xT, w_words, w_scales, b, gate, pos1, pos2, pos3, pos4, pos5, pos6, pos7, pos8):
    w = unpack_weight(w_words, w_scales)
    y = w.T @ mxq(f64(xT), 0, "e4m3")
    y = relu(y + f64(b))
    return sum(f64(gate[d]) * y[:, unstriped(p)] for d, p in enumerate((pos1, pos2, pos3, pos4, pos5, pos6, pos7, pos8)))

@@ -1,0 +1,166 @@
+from contextlib import ExitStack
+
+import concourse.mybir as mybir
+from concourse.masks import make_identity
+
+K, T, D, V, N = 1024, 512, 8, 256, 512
+FLOPS = 2 * K * N * T + 2 * D * N * V
+
+F32 = mybir.dt.float32
+BF16 = mybir.dt.bfloat16
+I32 = mybir.dt.int32
+U32 = mybir.dt.uint32
+U16 = mybir.dt.uint16
+U8 = mybir.dt.uint8
+FP8X4 = mybir.dt.float8_e4m3fn_x4
+RELU = mybir.ActivationFunctionType.Relu
+MULT = mybir.AluOpType.mult
+ADD = mybir.AluOpType.add
+
+P = 128
+PACK = 4
+K_PASS = P * PACK
+PASSES = K // K_PASS
+M_TILES = N // P
+V_BLOCKS = V // P
+CHUNKS = ((0, 0, 256, 144), (1, 0, 256, 144), (0, 256, 512, 144), (1, 256, 384, 80), (1, 384, 512, 80))
+GROUPS = ((0, 256), (256, 384), (384, 512))
+
+
+def tile_picked_agg_lin_relu_sub_l_kernel(
+    tc, xT, w_words, w_scales, b, gate, pos1, pos2, pos3, pos4, pos5, pos6, pos7, pos8, out
+):
+    nc = tc.nc
+    lists = (pos1, pos2, pos3, pos4, pos5, pos6, pos7, pos8)
+
+    with ExitStack() as ctx:
+        keep = ctx.enter_context(tc.tile_pool(name="keep", bufs=1))
+        psum = ctx.enter_context(tc.psum_pool(name="psum", bufs=8))
+
+        offsets = [keep.tile([P, V // 16], U16, name=f"offsets{d}") for d in range(D)]
+        w_scale = keep.tile([P, PASSES, N], U8, name="w_scale", align_bytes=64)
+        warm = keep.tile([P, 8], F32, name="warm")
+        warm_out = keep.tile([P, 8], F32, name="warm_out")
+        bias = keep.tile([P, M_TILES], F32, name="bias")
+        ident = keep.tile([P, P], F32, name="ident")
+        w_first = keep.tile([P, PASSES, P], U32, name="w_first", align_bytes=64)
+        w_rest = keep.tile([P, PASSES, N - P], U32, name="w_rest", align_bytes=64)
+        x_codes = keep.tile([P, PASSES, T], U32, name="x_codes", align_bytes=64)
+        x_scale = keep.tile([P, PASSES, T], U8, name="x_scale", align_bytes=64)
+        raw = [keep.tile([P, PACK, c1 - c0], F32, name=f"raw{a}_{c0}") for a, c0, c1, cut in CHUNKS]
+        grouped = [keep.tile([P, c1 - c0, PACK], BF16, name=f"grouped{a}_{c0}", align_bytes=64) for a, c0, c1, cut in CHUNKS]
+        gates = [keep.tile([P, D, V], F32, name=f"gates{j}") for j in range(M_TILES)]
+        y = [keep.tile([P, T], F32, name=f"y{j}") for j in range(M_TILES)]
+
+        nc.vector.memset(w_scale[:].rearrange("p a n -> p (a n)").bitcast(U32), 0)
+        nc.vector.memset(warm[:], 0.0)
+
+        words = w_words.rearrange("a p n t -> p a (n t)")
+        gate_rows = gate.rearrange("d (j p) v -> j p d v", p=P)
+        for c, (a, c0, c1, cut) in enumerate(CHUNKS):
+            rows = xT[a * K_PASS : (a + 1) * K_PASS, c0:c1]
+            nc.sync.dma_start(out=raw[c][:], in_=rows.rearrange("(p j) w -> p j w", j=PACK))
+            if c == 1:
+                nc.sync.dma_start(out=w_first[:].bitcast(I32), in_=words[:, :, 0 : P * PACK].bitcast(I32))
+        scale_rows = w_scales.rearrange("a (q r) n -> r q a n", r=4)
+        for r in range(4):
+            nc.scalar.dma_start(out=w_scale[r:P:32, :, :].bitcast(I32), in_=scale_rows[r].bitcast(I32))
+        with nc.allow_non_contiguous_dma(reason="one bias value to a partition"):
+            nc.scalar.dma_start(out=bias[:], in_=b.rearrange("(j p) o -> p (j o)", p=P))
+        nc.scalar.activation(out=warm_out[:], in_=warm[:], func=RELU, bias=warm[:, 0:1])
+
+        nc.sync.dma_start(offsets[0][:], lists[0])
+        nc.sync.dma_start(out=gates[0][:, 0:2, :], in_=gate_rows[0][:, 0:2, :])
+        nc.sync.dma_start(offsets[1][:], lists[1])
+        nc.sync.dma_start(offsets[2][:], lists[2])
+        nc.sync.dma_start(out=gates[0][:, 2:D, :], in_=gate_rows[0][:, 2:D, :])
+        for d in range(3, D):
+            nc.sync.dma_start(offsets[d][:], lists[d])
+        nc.sync.dma_start(out=w_rest[:].bitcast(I32), in_=words[:, :, P * PACK : N * PACK].bitcast(I32))
+        for j in range(1, M_TILES):
+            nc.sync.dma_start(out=gates[j][:], in_=gate_rows[j])
+
+        make_identity(nc, ident[:])
+
+        def project(acc, j, a, c0, c1):
+            if j == 0:
+                w = w_first[:, a, :]
+            else:
+                w = w_rest[:, a, (j - 1) * P : j * P]
+            nc.tensor.matmul_mx(
+                out=acc[:, 0 : c1 - c0],
+                lhsT=w.bitcast(FP8X4),
+                lhsT_scale=w_scale[:, a, j * P : (j + 1) * P],
+                rhs=x_codes[:, a, c0:c1].bitcast(FP8X4),
+                rhs_scale=x_scale[:, a, c0:c1],
+                start=(a == 0),
+                stop=(a == PASSES - 1),
+            )
+
+        first = {g: psum.tile([P, T], F32, name="bank") for g in GROUPS}
+        for c, (a, c0, c1, cut) in enumerate(CHUNKS):
+            src = raw[c][:].rearrange("p t (c i) -> p c t i", i=4)
+            dst = grouped[c][:].rearrange("p (c i) t -> p c t i", i=4)
+            nc.vector.tensor_copy(out=dst[:, 0 : cut // 4], in_=src[:, 0 : cut // 4])
+            nc.scalar.copy(out=dst[:, cut // 4 :], in_=src[:, cut // 4 :])
+            nc.vector.quantize_mx(
+                out=x_codes[:, a, c0:c1].bitcast(FP8X4),
+                scales=x_scale[:, a, c0:c1],
+                in_=grouped[c][:].rearrange("p w t -> p (w t)"),
+            )
+            for g0, g1 in GROUPS:
+                if c0 <= g0 and g1 <= c1:
+                    acc = first[g0, g1]
+                    project(acc, 0, a, g0, g1)
+                    if a == PASSES - 1:
+                        nc.scalar.activation(out=y[0][:, g0:g1], in_=acc[:, 0 : g1 - g0], func=RELU, bias=bias[:, 0:1])
+
+        for j in range(1, M_TILES):
+            acc = psum.tile([P, T], F32, name="bank")
+            for a in range(PASSES):
+                project(acc, j, a, 0, T)
+            nc.scalar.activation(out=y[j][:], in_=acc[:], func=RELU, bias=bias[:, j : j + 1])
+
+        terms = {(j, d): keep.tile([P, V], F32, name=f"term{j}_{d}") for j in range(M_TILES) for d in range(D)}
+        result = [keep.tile([P, V], F32, name=f"result{j}") for j in range(M_TILES)]
+
+        def gather(j, d):
+            nc.vector.tensor_tensor(terms[j, d][:], y[j][:].indirect(offsets[d][:]), gates[j][:, d, :], MULT)
+
+        def gather_and_sum(j, count):
+            turned = psum.tile([P, T], F32, name="bank")
+            for d in range(count):
+                gather(j, d)
+                for u in range(V_BLOCKS):
+                    nc.tensor.matmul(
+                        turned[:, u * P : (u + 1) * P],
+                        lhsT=terms[j, d][:, u * P : (u + 1) * P],
+                        rhs=ident[:],
+                        start=(d == 0 and u == 0),
+                        stop=(d == count - 1 and u == V_BLOCKS - 1),
+                        is_transpose=True,
+                    )
+            turned_sb = keep.tile([P, V], F32, name=f"turned_sb{j}")
+            nc.scalar.copy(out=turned_sb[:], in_=turned[:, 0:V])
+            back = psum.tile([P, T], F32, name="bank")
+            for u in range(V_BLOCKS):
+                nc.tensor.transpose(back[:, u * P : (u + 1) * P], turned_sb[:, u * P : (u + 1) * P], ident[:])
+            return back
+
+        def store(j):
+            nc.sync.dma_start(out=out[j * P : (j + 1) * P, :], in_=result[j][:])
+
+        late = (M_TILES - 2, M_TILES - 1)
+        partial = {}
+        for j in range(M_TILES):
+            if j in late:
+                partial[j] = gather_and_sum(j, D - 1)
+            else:
+                back = gather_and_sum(j, D)
+                nc.scalar.copy(out=result[j][:], in_=back[:, 0:V])
+                store(j)
+        for j in late:
+            gather(j, D - 1)
+        for j in late:
+            nc.vector.tensor_tensor(result[j][:], partial[j][:, 0:V], terms[j, D - 1][:], ADD)
+            store(j)

@@ -41,7 +41,8 @@ def tile_picked_agg_lin_relu_sub_l_kernel(
         w_scale = keep.tile([P, PASSES, N], U8, name="w_scale", align_bytes=64)
         warm = keep.tile([P, 8], F32, name="warm")
         warm_out = keep.tile([P, 8], F32, name="warm_out")
-        bias = keep.tile([P, M_TILES], F32, name="bias")
+        bias_first = keep.tile([P, 1], F32, name="bias_first")
+        bias_rest = keep.tile([P, M_TILES - 1], F32, name="bias_rest")
         ident = keep.tile([P, P], F32, name="ident")
         w_first = keep.tile([P, PASSES, P], U32, name="w_first", align_bytes=64)
         w_rest = keep.tile([P, PASSES, N - P], U32, name="w_rest", align_bytes=64)
@@ -52,33 +53,44 @@ def tile_picked_agg_lin_relu_sub_l_kernel(
         gates = [keep.tile([P, D, V], F32, name=f"gates{j}") for j in range(M_TILES)]
         y = [keep.tile([P, T], F32, name=f"y{j}") for j in range(M_TILES)]
 
-        nc.vector.memset(w_scale[:].rearrange("p a n -> p (a n)").bitcast(U32), 0)
+        nc.gpsimd.memset(w_scale[:].rearrange("p a n -> p (a n)").bitcast(U32), 0)
         nc.vector.memset(warm[:], 0.0)
 
         words = w_words.rearrange("a p n t -> p a (n t)")
         gate_rows = gate.rearrange("d (j p) v -> j p d v", p=P)
+        scale_rows = w_scales.rearrange("a (q r) n -> r q a n", r=4)
+        bias_cols = b.rearrange("(j p) o -> p (j o)", p=P)
         for c, (a, c0, c1, cut) in enumerate(CHUNKS):
             rows = xT[a * K_PASS : (a + 1) * K_PASS, c0:c1]
             nc.sync.dma_start(out=raw[c][:], in_=rows.rearrange("(p j) w -> p j w", j=PACK))
             if c == 1:
                 nc.sync.dma_start(out=w_first[:].bitcast(I32), in_=words[:, :, 0 : P * PACK].bitcast(I32))
-        scale_rows = w_scales.rearrange("a (q r) n -> r q a n", r=4)
-        for r in range(4):
-            nc.scalar.dma_start(out=w_scale[r:P:32, :, :].bitcast(I32), in_=scale_rows[r].bitcast(I32))
-        with nc.allow_non_contiguous_dma(reason="one bias value to a partition"):
-            nc.scalar.dma_start(out=bias[:], in_=b.rearrange("(j p) o -> p (j o)", p=P))
+                nc.sync.dma_start(out=bias_first[:], in_=b[0:P, :])
+                for r in range(4):
+                    nc.sync.dma_start(out=w_scale[r:P:32, :, :].bitcast(I32), in_=scale_rows[r].bitcast(I32))
         nc.scalar.activation(out=warm_out[:], in_=warm[:], func=RELU, bias=warm[:, 0:1])
 
-        nc.sync.dma_start(offsets[0][:], lists[0])
-        nc.sync.dma_start(out=gates[0][:, 0:2, :], in_=gate_rows[0][:, 0:2, :])
-        nc.sync.dma_start(offsets[1][:], lists[1])
-        nc.sync.dma_start(offsets[2][:], lists[2])
-        nc.sync.dma_start(out=gates[0][:, 2:D, :], in_=gate_rows[0][:, 2:D, :])
-        for d in range(3, D):
-            nc.sync.dma_start(offsets[d][:], lists[d])
+        def load_gates(j, d0, d1):
+            nc.sync.dma_start(out=gates[j][:, d0:d1, :], in_=gate_rows[j][:, d0:d1, :])
+
+        def load_lists(d0, d1):
+            for d in range(d0, d1):
+                nc.sync.dma_start(offsets[d][:], lists[d])
+
+        load_lists(0, 1)
+        load_gates(0, 0, 2)
+        load_lists(1, 3)
+        load_gates(0, 2, 5)
+        load_lists(3, 5)
         nc.sync.dma_start(out=w_rest[:].bitcast(I32), in_=words[:, :, P * PACK : N * PACK].bitcast(I32))
-        for j in range(1, M_TILES):
-            nc.sync.dma_start(out=gates[j][:], in_=gate_rows[j])
+        load_lists(5, D)
+        load_gates(0, 5, D)
+        with nc.allow_non_contiguous_dma(reason="one bias value to a partition"):
+            nc.sync.dma_start(out=bias_rest[:], in_=bias_cols[:, 1:M_TILES])
+        load_gates(1, 0, D // 2)
+        load_gates(1, D // 2, D)
+        for j in range(2, M_TILES):
+            load_gates(j, 0, D)
 
         make_identity(nc, ident[:])
 
@@ -113,13 +125,13 @@ def tile_picked_agg_lin_relu_sub_l_kernel(
                     acc = first[g0, g1]
                     project(acc, 0, a, g0, g1)
                     if a == PASSES - 1:
-                        nc.scalar.activation(out=y[0][:, g0:g1], in_=acc[:, 0 : g1 - g0], func=RELU, bias=bias[:, 0:1])
+                        nc.scalar.activation(out=y[0][:, g0:g1], in_=acc[:, 0 : g1 - g0], func=RELU, bias=bias_first[:])
 
         for j in range(1, M_TILES):
             acc = psum.tile([P, T], F32, name="bank")
             for a in range(PASSES):
                 project(acc, j, a, 0, T)
-            nc.scalar.activation(out=y[j][:], in_=acc[:], func=RELU, bias=bias[:, j : j + 1])
+            nc.scalar.activation(out=y[j][:], in_=acc[:], func=RELU, bias=bias_rest[:, j - 1 : j])
 
         terms = {(j, d): keep.tile([P, V], F32, name=f"term{j}_{d}") for j in range(M_TILES) for d in range(D)}
         result = [keep.tile([P, V], F32, name=f"result{j}") for j in range(M_TILES)]
@@ -127,40 +139,41 @@ def tile_picked_agg_lin_relu_sub_l_kernel(
         def gather(j, d):
             nc.vector.tensor_tensor(terms[j, d][:], y[j][:].indirect(offsets[d][:]), gates[j][:, d, :], MULT)
 
-        def gather_and_sum(j, count):
-            turned = psum.tile([P, T], F32, name="bank")
+        def gather_and_sum(j, count, spans):
+            turned = [psum.tile([P, T], F32, name="bank") for span in spans]
             for d in range(count):
                 gather(j, d)
-                for u in range(V_BLOCKS):
-                    nc.tensor.matmul(
-                        turned[:, u * P : (u + 1) * P],
-                        lhsT=terms[j, d][:, u * P : (u + 1) * P],
-                        rhs=ident[:],
-                        start=(d == 0 and u == 0),
-                        stop=(d == count - 1 and u == V_BLOCKS - 1),
-                        is_transpose=True,
-                    )
+                for bank, span in zip(turned, spans):
+                    for u in span:
+                        nc.tensor.matmul(
+                            bank[:, u * P : (u + 1) * P],
+                            lhsT=terms[j, d][:, u * P : (u + 1) * P],
+                            rhs=ident[:],
+                            start=(d == 0 and u == span[0]),
+                            stop=(d == count - 1 and u == span[-1]),
+                            is_transpose=True,
+                        )
             turned_sb = keep.tile([P, V], F32, name=f"turned_sb{j}")
-            nc.scalar.copy(out=turned_sb[:], in_=turned[:, 0:V])
-            back = psum.tile([P, T], F32, name="bank")
-            for u in range(V_BLOCKS):
-                nc.tensor.transpose(back[:, u * P : (u + 1) * P], turned_sb[:, u * P : (u + 1) * P], ident[:])
+            back = [psum.tile([P, T], F32, name="bank") for span in spans]
+            for bank, home, span in zip(turned, back, spans):
+                cols = slice(span[0] * P, (span[-1] + 1) * P)
+                nc.scalar.copy(out=turned_sb[:, cols], in_=bank[:, cols])
+                for u in span:
+                    nc.tensor.transpose(home[:, u * P : (u + 1) * P], turned_sb[:, u * P : (u + 1) * P], ident[:])
             return back
 
-        def store(j):
+        whole = (range(V_BLOCKS),)
+        halves = tuple(range(u, u + 1) for u in range(V_BLOCKS))
+        for j in range(M_TILES - 2):
+            back = gather_and_sum(j, D, whole)
+            nc.scalar.copy(out=result[j][:], in_=back[0][:, 0:V])
             nc.sync.dma_start(out=out[j * P : (j + 1) * P, :], in_=result[j][:])
-
-        late = (M_TILES - 2, M_TILES - 1)
-        partial = {}
-        for j in range(M_TILES):
-            if j in late:
-                partial[j] = gather_and_sum(j, D - 1)
-            else:
-                back = gather_and_sum(j, D)
-                nc.scalar.copy(out=result[j][:], in_=back[:, 0:V])
-                store(j)
+        late = {M_TILES - 2: whole, M_TILES - 1: halves}
+        partial = {j: gather_and_sum(j, D - 1, spans) for j, spans in late.items()}
         for j in late:
             gather(j, D - 1)
-        for j in late:
-            nc.vector.tensor_tensor(result[j][:], partial[j][:, 0:V], terms[j, D - 1][:], ADD)
-            store(j)
+        for j, spans in late.items():
+            for home, span in zip(partial[j], spans):
+                cols = slice(span[0] * P, (span[-1] + 1) * P)
+                nc.vector.tensor_tensor(result[j][:, cols], home[:, cols], terms[j, D - 1][:, cols], ADD)
+                nc.sync.dma_start(out=out[j * P : (j + 1) * P, cols], in_=result[j][:, cols])

@@ -23,7 +23,7 @@ K_PASS = P * PACK
 PASSES = K // K_PASS
 M_TILES = N // P
 V_BLOCKS = V // P
-CHUNKS = ((0, 0, 256, 144), (1, 0, 256, 144), (0, 256, 512, 144), (1, 256, 384, 80), (1, 384, 512, 80))
+CHUNKS = ((0, 0, 256, 160), (0, 256, 512, 160), (1, 0, 256, 160), (1, 256, 384, 88), (1, 384, 512, 88))
 GROUPS = ((0, 256), (256, 384), (384, 512))
 
 
@@ -55,6 +55,7 @@ def tile_picked_agg_lin_relu_sub_l_kernel(
 
         nc.gpsimd.memset(w_scale[:].rearrange("p a n -> p (a n)").bitcast(U32), 0)
         nc.vector.memset(warm[:], 0.0)
+        nc.gpsimd.dma_start(out=bias_first[:], in_=b[0:P, :])
 
         words = w_words.rearrange("a p n t -> p a (n t)")
         gate_rows = gate.rearrange("d (j p) v -> j p d v", p=P)
@@ -65,7 +66,6 @@ def tile_picked_agg_lin_relu_sub_l_kernel(
             nc.sync.dma_start(out=raw[c][:], in_=rows.rearrange("(p j) w -> p j w", j=PACK))
             if c == 1:
                 nc.sync.dma_start(out=w_first[:].bitcast(I32), in_=words[:, :, 0 : P * PACK].bitcast(I32))
-                nc.sync.dma_start(out=bias_first[:], in_=b[0:P, :])
                 for r in range(4):
                     nc.sync.dma_start(out=w_scale[r:P:32, :, :].bitcast(I32), in_=scale_rows[r].bitcast(I32))
         nc.scalar.activation(out=warm_out[:], in_=warm[:], func=RELU, bias=warm[:, 0:1])

from contextlib import ExitStack

import concourse.mybir as mybir
from concourse.masks import make_identity

K, T, D, V, N = 1024, 512, 8, 256, 512
FLOPS = 2 * K * N * T + 2 * D * N * V

F32 = mybir.dt.float32
BF16 = mybir.dt.bfloat16
I32 = mybir.dt.int32
U32 = mybir.dt.uint32
U16 = mybir.dt.uint16
U8 = mybir.dt.uint8
FP8X4 = mybir.dt.float8_e4m3fn_x4
RELU = mybir.ActivationFunctionType.Relu
MULT = mybir.AluOpType.mult
ADD = mybir.AluOpType.add

P = 128
PACK = 4
K_PASS = P * PACK
PASSES = K // K_PASS
M_TILES = N // P
V_BLOCKS = V // P
CHUNKS = ((0, 0, 256, 160), (0, 256, 512, 160), (1, 0, 256, 160), (1, 256, 384, 88), (1, 384, 512, 88))
GROUPS = ((0, 256), (256, 384), (384, 512))


def tile_picked_agg_lin_relu_sub_l_kernel(
    tc, xT, w_words, w_scales, b, gate, pos1, pos2, pos3, pos4, pos5, pos6, pos7, pos8, out
):
    nc = tc.nc
    lists = (pos1, pos2, pos3, pos4, pos5, pos6, pos7, pos8)

    with ExitStack() as ctx:
        keep = ctx.enter_context(tc.tile_pool(name="keep", bufs=1))
        psum = ctx.enter_context(tc.psum_pool(name="psum", bufs=8))

        offsets = [keep.tile([P, V // 16], U16, name=f"offsets{d}") for d in range(D)]
        w_scale = keep.tile([P, PASSES, N], U8, name="w_scale", align_bytes=64)
        warm = keep.tile([P, 8], F32, name="warm")
        warm_out = keep.tile([P, 8], F32, name="warm_out")
        bias_first = keep.tile([P, 1], F32, name="bias_first")
        bias_rest = keep.tile([P, M_TILES - 1], F32, name="bias_rest")
        ident = keep.tile([P, P], F32, name="ident")
        w_first = keep.tile([P, PASSES, P], U32, name="w_first", align_bytes=64)
        w_rest = keep.tile([P, PASSES, N - P], U32, name="w_rest", align_bytes=64)
        x_codes = keep.tile([P, PASSES, T], U32, name="x_codes", align_bytes=64)
        x_scale = keep.tile([P, PASSES, T], U8, name="x_scale", align_bytes=64)
        raw = [keep.tile([P, PACK, c1 - c0], F32, name=f"raw{a}_{c0}") for a, c0, c1, cut in CHUNKS]
        grouped = [keep.tile([P, c1 - c0, PACK], BF16, name=f"grouped{a}_{c0}", align_bytes=64) for a, c0, c1, cut in CHUNKS]
        gates = [keep.tile([P, D, V], F32, name=f"gates{j}") for j in range(M_TILES)]
        y = [keep.tile([P, T], F32, name=f"y{j}") for j in range(M_TILES)]

        nc.gpsimd.memset(w_scale[:].rearrange("p a n -> p (a n)").bitcast(U32), 0)
        nc.vector.memset(warm[:], 0.0)
        nc.gpsimd.dma_start(out=bias_first[:], in_=b[0:P, :])

        words = w_words.rearrange("a p n t -> p a (n t)")
        gate_rows = gate.rearrange("d (j p) v -> j p d v", p=P)
        scale_rows = w_scales.rearrange("a (q r) n -> r q a n", r=4)
        bias_cols = b.rearrange("(j p) o -> p (j o)", p=P)
        for c, (a, c0, c1, cut) in enumerate(CHUNKS):
            rows = xT[a * K_PASS : (a + 1) * K_PASS, c0:c1]
            nc.sync.dma_start(out=raw[c][:], in_=rows.rearrange("(p j) w -> p j w", j=PACK))
            if c == 1:
                nc.sync.dma_start(out=w_first[:].bitcast(I32), in_=words[:, :, 0 : P * PACK].bitcast(I32))
                for r in range(4):
                    nc.sync.dma_start(out=w_scale[r:P:32, :, :].bitcast(I32), in_=scale_rows[r].bitcast(I32))
        nc.scalar.activation(out=warm_out[:], in_=warm[:], func=RELU, bias=warm[:, 0:1])

        def load_gates(j, d0, d1):
            nc.sync.dma_start(out=gates[j][:, d0:d1, :], in_=gate_rows[j][:, d0:d1, :])

        def load_lists(d0, d1):
            for d in range(d0, d1):
                nc.sync.dma_start(offsets[d][:], lists[d])

        load_lists(0, 1)
        load_gates(0, 0, 2)
        load_lists(1, 3)
        load_gates(0, 2, 5)
        load_lists(3, 5)
        nc.sync.dma_start(out=w_rest[:].bitcast(I32), in_=words[:, :, P * PACK : N * PACK].bitcast(I32))
        load_lists(5, D)
        load_gates(0, 5, D)
        with nc.allow_non_contiguous_dma(reason="one bias value to a partition"):
            nc.sync.dma_start(out=bias_rest[:], in_=bias_cols[:, 1:M_TILES])
        load_gates(1, 0, D // 2)
        load_gates(1, D // 2, D)
        for j in range(2, M_TILES):
            load_gates(j, 0, D)

        make_identity(nc, ident[:])

        def project(acc, j, a, c0, c1):
            if j == 0:
                w = w_first[:, a, :]
            else:
                w = w_rest[:, a, (j - 1) * P : j * P]
            nc.tensor.matmul_mx(
                out=acc[:, 0 : c1 - c0],
                lhsT=w.bitcast(FP8X4),
                lhsT_scale=w_scale[:, a, j * P : (j + 1) * P],
                rhs=x_codes[:, a, c0:c1].bitcast(FP8X4),
                rhs_scale=x_scale[:, a, c0:c1],
                start=(a == 0),
                stop=(a == PASSES - 1),
            )

        first = {g: psum.tile([P, T], F32, name="bank") for g in GROUPS}
        for c, (a, c0, c1, cut) in enumerate(CHUNKS):
            src = raw[c][:].rearrange("p t (c i) -> p c t i", i=4)
            dst = grouped[c][:].rearrange("p (c i) t -> p c t i", i=4)
            nc.vector.tensor_copy(out=dst[:, 0 : cut // 4], in_=src[:, 0 : cut // 4])
            nc.scalar.copy(out=dst[:, cut // 4 :], in_=src[:, cut // 4 :])
            nc.vector.quantize_mx(
                out=x_codes[:, a, c0:c1].bitcast(FP8X4),
                scales=x_scale[:, a, c0:c1],
                in_=grouped[c][:].rearrange("p w t -> p (w t)"),
            )
            for g0, g1 in GROUPS:
                if c0 <= g0 and g1 <= c1:
                    acc = first[g0, g1]
                    project(acc, 0, a, g0, g1)
                    if a == PASSES - 1:
                        nc.scalar.activation(out=y[0][:, g0:g1], in_=acc[:, 0 : g1 - g0], func=RELU, bias=bias_first[:])

        for j in range(1, M_TILES):
            acc = psum.tile([P, T], F32, name="bank")
            for a in range(PASSES):
                project(acc, j, a, 0, T)
            nc.scalar.activation(out=y[j][:], in_=acc[:], func=RELU, bias=bias_rest[:, j - 1 : j])

        terms = {(j, d): keep.tile([P, V], F32, name=f"term{j}_{d}") for j in range(M_TILES) for d in range(D)}
        result = [keep.tile([P, V], F32, name=f"result{j}") for j in range(M_TILES)]

        def gather(j, d):
            nc.vector.tensor_tensor(terms[j, d][:], y[j][:].indirect(offsets[d][:]), gates[j][:, d, :], MULT)

        def gather_and_sum(j, count, spans):
            turned = [psum.tile([P, T], F32, name="bank") for span in spans]
            for d in range(count):
                gather(j, d)
                for bank, span in zip(turned, spans):
                    for u in span:
                        nc.tensor.matmul(
                            bank[:, u * P : (u + 1) * P],
                            lhsT=terms[j, d][:, u * P : (u + 1) * P],
                            rhs=ident[:],
                            start=(d == 0 and u == span[0]),
                            stop=(d == count - 1 and u == span[-1]),
                            is_transpose=True,
                        )
            turned_sb = keep.tile([P, V], F32, name=f"turned_sb{j}")
            back = [psum.tile([P, T], F32, name="bank") for span in spans]
            for bank, home, span in zip(turned, back, spans):
                cols = slice(span[0] * P, (span[-1] + 1) * P)
                nc.scalar.copy(out=turned_sb[:, cols], in_=bank[:, cols])
                for u in span:
                    nc.tensor.transpose(home[:, u * P : (u + 1) * P], turned_sb[:, u * P : (u + 1) * P], ident[:])
            return back

        whole = (range(V_BLOCKS),)
        halves = tuple(range(u, u + 1) for u in range(V_BLOCKS))
        for j in range(M_TILES - 2):
            back = gather_and_sum(j, D, whole)
            nc.scalar.copy(out=result[j][:], in_=back[0][:, 0:V])
            nc.sync.dma_start(out=out[j * P : (j + 1) * P, :], in_=result[j][:])
        late = {M_TILES - 2: whole, M_TILES - 1: halves}
        partial = {j: gather_and_sum(j, D - 1, spans) for j, spans in late.items()}
        for j in late:
            gather(j, D - 1)
        for j, spans in late.items():
            for home, span in zip(partial[j], spans):
                cols = slice(span[0] * P, (span[-1] + 1) * P)
                nc.vector.tensor_tensor(result[j][:, cols], home[:, cols], terms[j, D - 1][:, cols], ADD)
                nc.sync.dma_start(out=out[j * P : (j + 1) * P, cols], in_=result[j][:, cols])
